import numpy as np
import ml_dtypes


def mxq(x, axis, fmt="e4m3"):
    dtype, down = {"e4m3": (ml_dtypes.float8_e4m3fn, 7), "e5m2": (ml_dtypes.float8_e5m2, 14)}[fmt]
    v = np.moveaxis(np.asarray(x, np.float32).astype(ml_dtypes.bfloat16).astype(np.float64), axis, -1)
    blocks = v.reshape(v.shape[:-1] + (-1, 32))
    amax = np.abs(blocks).max(-1, keepdims=True)
    byte = np.maximum(np.where(amax > 0, np.frexp(amax)[1] - 1 + 127, 0) - down, 1)
    scale = np.exp2(byte - 127.0)
    codes = (blocks / scale).astype(np.float32).astype(dtype).astype(np.float64)
    return np.moveaxis((codes * scale).reshape(v.shape), -1, axis)


WIDE = False


def mx_kscale(k):
    if not WIDE:
        return np.ones(k)
    levels = np.array([10, -10, 5, -5, 0])
    if k % 512:
        return np.exp2(np.random.permutation(np.resize(levels, k // 32))).repeat(32)
    a = np.empty((k // 512, 16))
    for p in range(k // 512):
        a[p, :8] = np.random.permutation(np.resize(levels, 8))
        for g in range(8):
            far = levels[np.abs(levels - a[p, g]) >= 10]
            a[p, g + 8] = far[np.random.randint(len(far))]
    return np.exp2(a.ravel()).repeat(32)


def f64(x):
    return np.asarray(x).astype(np.float64)


def striped(idx):
    return np.tile(idx.reshape(-1, 16).T, (8, 1)).astype(np.uint16)


def unstriped(offs):
    return offs[:16].T.reshape(-1).astype(np.int64)


E2M1 = np.array([0.0, 0.5, 1.0, 1.5, 2.0, 3.0, 4.0, 6.0, -0.0, -0.5, -1.0, -1.5, -2.0, -3.0, -4.0, -6.0])


def pack_weight(w, fmt):
    k, n = w.shape
    w = f64(np.asarray(w, np.float32).astype(ml_dtypes.bfloat16)).reshape(k // 32, 32, n)
    amax = np.abs(w).max(1)
    if fmt == "e4m3":
        byte = np.frexp(amax)[1] - 1 + 127 - 7
    else:
        mant, ex = np.frexp(amax / 6.0)
        byte = np.where(mant > 0.5, ex, ex - 1) + 127
    byte = np.clip(np.where(amax > 0, byte, 1), 1, 254)
    scaled = (w * np.exp2(127.0 - byte)[:, None, :]).reshape(k, n).astype(np.float32)
    by_word = np.ascontiguousarray(scaled.reshape(k // 512, 128, 4, n).transpose(0, 1, 3, 2))
    if fmt == "e4m3":
        words = by_word.astype(ml_dtypes.float8_e4m3fn).view(np.uint8)
    else:
        c = by_word.astype(ml_dtypes.float4_e2m1fn).view(np.uint8) & 0xF
        words = (c[..., 0::2] | (c[..., 1::2] << 4)).reshape(k // 512, 128, 2 * n)
    return np.ascontiguousarray(words), np.ascontiguousarray(byte.astype(np.uint8).reshape(k // 512, 16, n))


def unpack_weight(words, scales, fmt):
    g, _, n = scales.shape
    words = np.ascontiguousarray(words).reshape(g, 128, n, -1)
    if fmt == "e4m3":
        vals = words.view(ml_dtypes.float8_e4m3fn).astype(np.float64)
    else:
        nib = np.empty((g, 128, n, 4), np.uint8)
        nib[..., 0::2] = words & 0xF
        nib[..., 1::2] = words >> 4
        vals = E2M1[nib]
    vals = vals * np.repeat(np.exp2(scales.astype(np.float64) - 127.0), 8, axis=1)[..., None]
    return vals.transpose(0, 1, 3, 2).reshape(g * 512, n)


def gelu(v):
    return 0.5 * v * (1.0 + np.tanh(np.sqrt(2.0 / np.pi) * (v + 0.044715 * v**3)))


def striped8(idx):
    return np.concatenate([v.reshape(-1, 16).T for v in idx]).astype(np.uint16)


def unstriped8(offs):
    return np.stack([offs[16 * g:16 * g + 16].T.reshape(-1) for g in range(8)]).astype(np.int64)


def runs(v, idx8):
    k = np.arange(v.shape[0])
    return v[k[:, None], idx8[k % 512 // 64]]


K, M, H, N, T, S, T2 = 1024, 512, 512, 384, 2048, 1024, 2048


def setup_inputs():
    n = np.random.standard_normal
    s = mx_kscale(K)[:, None]
    s2 = mx_kscale(M)[:, None]
    u = mx_kscale(H)[:, None]
    tab_words, tab_scales = pack_weight(n((K, T)) * s, "e4m3")
    tab2_words, tab2_scales = pack_weight(n((M, T)) * s2, "e4m3")
    wfs_words, wfs_scales = pack_weight(0.39 * n((K, H)) / np.sqrt(K) / s, "e2m1")
    wpc_words, wpc_scales = pack_weight(0.39 * n((M, H)) / np.sqrt(M) / s2, "e2m1")
    return {
        "tab_words": tab_words, "tab_scales": tab_scales,
        "tab2_words": tab2_words, "tab2_scales": tab2_scales,
        "offs": striped8(np.stack([np.random.permutation(T)[:S] for _ in range(8)])),
        "offs2": striped(np.random.permutation(T)[:S]),
        "offs3": striped(np.random.permutation(T2)[:S]),
        "wfc": (0.39 * n((K, H)) / np.sqrt(K) / s).astype(np.float32),
        "wpc_words": wpc_words, "wpc_scales": wpc_scales,
        "wfs_words": wfs_words, "wfs_scales": wfs_scales,
        "wps": (0.39 * n((M, H)) / np.sqrt(M) / s2).astype(np.float32),
        "gain": (np.exp(0.3 * n(H)) * u[:, 0]).astype(np.float32),
        "w5": (2.5 * n((H, N)) / np.sqrt(H) / u).astype(np.float32),
        "wgo": np.exp(0.3 * n((128, S))).astype(np.float32),
        "page1": n((N, T2)).astype(np.float32),
    }


def reference(tab_words, tab_scales, tab2_words, tab2_scales, offs, offs2, offs3, wfc, wpc_words, wpc_scales, wfs_words, wfs_scales, wps, gain, w5, wgo, page1):
    v = runs(unpack_weight(tab_words, tab_scales, "e4m3"), unstriped8(offs))
    v2 = unpack_weight(tab2_words, tab2_scales, "e4m3")[:, unstriped(offs2)]
    wpc = unpack_weight(wpc_words, wpc_scales, "e2m1")
    wfs = unpack_weight(wfs_words, wfs_scales, "e2m1")
    pc = mxq(f64(wfc), 0, "e4m3").T @ v + wpc.T @ v2
    ps = wfs.T @ v + mxq(f64(wps), 0, "e4m3").T @ v2
    z = np.cos(pc) * np.sin(ps) * f64(gain)[:, None]
    y = mxq(f64(w5), 0, "e4m3").T @ mxq(z, 0, "e4m3")
    out = f64(page1).copy()
    out[:, unstriped(offs3)] = np.tile(f64(wgo), (N // 128, 1)) * y
    return out

@@ -1,0 +1,250 @@
+import math
+from contextlib import ExitStack
+
+import concourse.mybir as mybir
+
+K, M, H, N, T, S, T2 = 1024, 512, 512, 384, 2048, 1024, 2048
+FLOPS = 2 * S * H * (2 * K + 2 * M) + 2 * S * H * N
+
+F32 = mybir.dt.float32
+BF16 = mybir.dt.bfloat16
+I32 = mybir.dt.int32
+U32 = mybir.dt.uint32
+U16 = mybir.dt.uint16
+U8 = mybir.dt.uint8
+E4M3 = mybir.dt.float8_e4m3fn_x4
+E2M1 = mybir.dt.float4_e2m1fn_x4
+ACT = mybir.ActivationFunctionType
+ALU = mybir.AluOpType
+
+P = 128
+CH = 256
+CHUNKS = S // CH
+QUARTER_PI_HI = round(math.pi / 4 * 2**24) / 2**24
+QUARTER_PI_LO = math.pi / 4 - QUARTER_PI_HI
+
+
+def tile_list_marker_slip_features_kernel(
+    tc, tab_words, tab_scales, tab2_words, tab2_scales, offs, offs2, offs3, wfc, wpc_words, wpc_scales,
+    wfs_words, wfs_scales, wps, gain, w5, wgo, page1, out,
+):
+    nc = tc.nc
+    with ExitStack() as ctx:
+        keep = ctx.enter_context(tc.tile_pool(name="keep", bufs=1))
+        ring = ctx.enter_context(tc.tile_pool(name="ring", bufs=2))
+        psum = ctx.enter_context(tc.psum_pool(name="psum", bufs=1))
+
+        def held(name, shape, dtype):
+            return keep.tile(shape, dtype, name=name, align_bytes=64)
+
+        list1 = held("list1", [P, S // 16], U16)
+        list2 = held("list2", [P, S // 16], U16)
+        list3 = held("list3", [P, S // 16], U16)
+        tab_sc = held("tab_sc", [P, T // 4], I32)
+        tab2_sc = held("tab2_sc", [P, T // 4], I32)
+        v_planes = held("v_planes", [P, 2 * S // 4], I32)
+        fs_sc_raw = held("fs_sc_raw", [P, 2 * H // 4], I32)
+        pc_sc_raw = held("pc_sc_raw", [P, H // 4], I32)
+        for zeroed in (tab_sc, tab2_sc, fs_sc_raw, pc_sc_raw, v_planes):
+            nc.vector.memset(zeroed[:], 0)
+
+        nc.sync.dma_start(list1[:], offs)
+        nc.sync.dma_start(out=tab_sc[0:P:4, :], in_=tab_scales.bitcast(I32).rearrange("a q w -> q a w"))
+        nc.sync.dma_start(list2[:], offs2)
+        for d in range(4):
+            nc.sync.dma_start(out=tab2_sc[32 * d : 32 * d + 4, :], in_=tab2_scales[0, 4 * d : 4 * d + 4, :].bitcast(I32))
+
+        def load_weight(name, rows):
+            raw = held(name, [P, 4 * H], F32)
+            nc.sync.dma_start(out=raw[:], in_=rows.rearrange("(p j) c -> p (j c)", j=4))
+            return raw
+
+        def load_table(name, words):
+            tile = held(name, [P, T], I32)
+            nc.sync.dma_start(out=tile[:], in_=words.rearrange("p t i -> p (t i)").bitcast(I32))
+            return tile
+
+        wps_raw = load_weight("wps_raw", wps)
+        wfc_raw = [load_weight("wfc_raw0", wfc[0:512, :])]
+        tab2_w = load_table("tab2_w", tab2_words[0])
+        fs_w_raw = held("fs_w_raw", [P, 2, H // 2], I32)
+        nc.sync.dma_start(out=fs_w_raw[:], in_=wfs_words.bitcast(I32).rearrange("a p w -> p a w"))
+        pc_w_raw = held("pc_w_raw", [P, H // 2], I32)
+        nc.sync.dma_start(out=pc_w_raw[:], in_=wpc_words[0].bitcast(I32))
+        for d in range(4):
+            nc.sync.dma_start(
+                out=fs_sc_raw[32 * d : 32 * d + 4, :],
+                in_=wfs_scales[:, 4 * d : 4 * d + 4, :].bitcast(I32).rearrange("a r w -> r a w"),
+            )
+        wfc_raw.append(load_weight("wfc_raw1", wfc[512:1024, :]))
+        for d in range(4):
+            nc.sync.dma_start(out=pc_sc_raw[32 * d : 32 * d + 4, :], in_=wpc_scales[0, 4 * d : 4 * d + 4, :].bitcast(I32))
+        tab_w = [load_table("tab_w0", tab_words[0]), load_table("tab_w1", tab_words[1])]
+        gains = [held("gain%d" % t, [P, 1], F32) for t in range(4)]
+        with nc.allow_non_contiguous_dma(reason="one gain for each partition and slice"):
+            for t in range(4):
+                nc.sync.dma_start(out=gains[t][:], in_=gain.rearrange("(q t i) -> t q i", t=4, i=8)[t])
+        w5_raw = held("w5_raw", [P, 4 * N], F32)
+        for t in range(4):
+            nc.sync.dma_start(out=w5_raw[:, t * N : (t + 1) * N], in_=w5.rearrange("(q t i) n -> t q i n", t=4, i=8)[t])
+        wgo_sb = held("wgo_sb", [P, S], F32)
+        nc.sync.dma_start(out=wgo_sb[:], in_=wgo)
+        nc.sync.dma_start(list3[:], offs3)
+        pages = []
+        for n in range(N // P):
+            page = held("page%d" % n, [P, T2], F32)
+            nc.sync.dma_start(out=page[:], in_=page1[n * P : (n + 1) * P, :])
+            pages.append(page)
+
+        ones = held("ones", [P, 1], F32)
+        nc.vector.memset(ones[:], 1.0)
+        phase = held("phase", [P, 1], F32)
+        nc.vector.tensor_scalar(phase[:], ones[:], -QUARTER_PI_HI, -QUARTER_PI_LO, ALU.mult, ALU.add)
+
+        v_sc_picked = held("v_sc_picked", [P, S], U8)
+        nc.vector.tensor_copy(v_sc_picked[:], tab_sc[:].bitcast(U8).indirect(list1[:]))
+        for d in range(4):
+            nc.gpsimd.dma_start(out=v_planes[32 * d : 32 * d + 4, :], in_=v_sc_picked[32 * d : 32 * d + 32 : 4, :].bitcast(I32))
+        v2_plane = held("v2_plane", [P, S], U8)
+        nc.vector.tensor_copy(v2_plane[:], tab2_sc[:].bitcast(U8).indirect(list2[:]))
+        v_plane = v_planes[:].bitcast(U8)
+
+        def round_weight(name, raw):
+            grouped = held(name, [P, 4 * H], BF16)
+            nc.scalar.copy(
+                out=grouped[:].rearrange("p (t q i j) -> p q t i j", t=4, i=8, j=4),
+                in_=raw[:].rearrange("p (j q t i) -> p q t i j", j=4, t=4, i=8),
+            )
+            return grouped
+
+        def quantise(name, grouped, width):
+            codes = held(name + "_codes", [P, width], U32)
+            scales = held(name + "_scales", [P, width], U8)
+            nc.vector.quantize_mx(out=codes[:].bitcast(E4M3), scales=scales[:], in_=grouped[:])
+            return codes, scales
+
+        def deal(name, raw, passes, run):
+            dealt = held(name, [P, passes * 64 * run], U32)
+            nc.scalar.copy(
+                out=dealt[:].rearrange("p (a t q w) -> p a t q w", a=passes, t=4, w=run),
+                in_=raw.bitcast(U32).rearrange("p (a q t w) -> p a t q w", a=passes, t=4, w=run),
+            )
+            return dealt[:].bitcast(U8)
+
+        def gather_words(name, table, offsets, c):
+            picked = held("%s_%d" % (name, c), [P, CH], U32)
+            nc.vector.tensor_copy(picked[:], table[:].bitcast(U32).indirect(offsets[:, c * CH // 16 : (c + 1) * CH // 16]))
+            return picked
+
+        wps_q = quantise("wps", round_weight("wps_bf", wps_raw), H)
+        v2 = [gather_words("v2", tab2_w, list2, c) for c in range(CHUNKS)]
+        wfc_q = [quantise("wfc0", round_weight("wfc0_bf", wfc_raw[0]), H)]
+        fs_w = deal("fs_w", fs_w_raw[:].rearrange("p a w -> p (a w)"), 2, 4)
+        pc_w = deal("pc_w", pc_w_raw[:], 1, 4)
+        fs_sc = deal("fs_sc", fs_sc_raw[:], 2, 2)
+        pc_sc = deal("pc_sc", pc_sc_raw[:], 1, 2)
+        wfc_q.append(quantise("wfc1", round_weight("wfc1_bf", wfc_raw[1]), H))
+        v = [[gather_words("v%d" % a, tab_w[a], list1, c) for c in range(CHUNKS)] for a in range(2)]
+        half_gains = held("half_gains", [P, 4], F32)
+        for t in range(4):
+            nc.vector.tensor_scalar(half_gains[:, t : t + 1], gains[t][:], -0.5, None, ALU.mult)
+        w5_bf = held("w5_bf", [P, 4 * N], BF16)
+        nc.vector.tensor_copy(
+            out=w5_bf[:].rearrange("p (n t) -> p n t", t=4), in_=w5_raw[:].rearrange("p (t n) -> p n t", t=4)
+        )
+        w5_codes, w5_scales = quantise("w5", w5_bf, N)
+
+        def e4m3_weight(q, t):
+            return q[0][:, t * P : (t + 1) * P].bitcast(E4M3), q[1][:, t * P : (t + 1) * P]
+
+        def e2m1_weight(words, scales, a, t):
+            c0 = a * H + t * P
+            return words[:, 2 * c0 : 2 * (c0 + P)].bitcast(E2M1), scales[:, c0 : c0 + P]
+
+        def moving(k, c, j0, width):
+            cols = slice(j0, j0 + width)
+            g0 = c * CH + j0
+            if k == 0:
+                return v2[c][:, cols].bitcast(E4M3), v2_plane[:, g0 : g0 + width]
+            a = k - 1
+            return v[a][c][:, cols].bitcast(E4M3), v_plane[:, a * S + g0 : a * S + g0 + width]
+
+        def pc_weight(k, t):
+            return e2m1_weight(pc_w, pc_sc, 0, t) if k == 0 else e4m3_weight(wfc_q[k - 1], t)
+
+        def ps_weight(k, t):
+            return e4m3_weight(wps_q, t) if k == 0 else e2m1_weight(fs_w, fs_sc, k - 1, t)
+
+        def phase_sums(bank, weight, slices, c, j0, width):
+            steps = [(k, u, t) for k in range(3) for u, t in enumerate(slices)]
+            for k, u, t in steps:
+                lhs, lhs_sc = weight(k, t)
+                rhs, rhs_sc = moving(k, c, j0, width)
+                nc.tensor.matmul_mx(
+                    out=bank[:, u * width : (u + 1) * width], lhsT=lhs, lhsT_scale=lhs_sc, rhs=rhs, rhs_scale=rhs_sc,
+                    start=(k, u, t) == steps[0], stop=(k, u, t) == steps[-1],
+                )
+
+        def first_stage(c):
+            half_cos = ring.tile([P, 4 * CH], F32, name="half_cos")
+            for h in range(2):
+                bank = psum.tile([P, 2 * CH], F32, name="pc_bank", bufs=3)
+                phase_sums(bank, pc_weight, (2 * h, 2 * h + 1), c, 0, CH)
+                nc.scalar.activation(half_cos[:, 2 * h * CH : 2 * (h + 1) * CH], bank[:], ACT.Sin, scale=0.5)
+            half_sin = ring.tile([P, 4 * CH], F32, name="half_sin")
+            for h in range(2):
+                bank = psum.tile([P, 4 * P], F32, name="ps_bank", bufs=3)
+                phase_sums(bank, ps_weight, (0, 1, 2, 3), c, h * P, P)
+                nc.scalar.activation(
+                    half_sin[:, 4 * h * P : 4 * (h + 1) * P].rearrange("p (j t) -> p j t", t=4),
+                    bank[:].rearrange("p (t j) -> p j t", t=4), ACT.Sin, bias=phase[:], scale=0.5,
+                )
+            cos_sq = ring.tile([P, 4 * CH], F32, name="cos_sq")
+            nc.scalar.activation(cos_sq[:], half_cos[:], ACT.Square)
+            cos_gain = ring.tile([P, 4 * CH], F32, name="cos_gain")
+            for t in range(4):
+                cols = slice(t * CH, (t + 1) * CH)
+                nc.scalar.activation(
+                    cos_gain[:, cols], cos_sq[:, cols], ACT.Identity, bias=half_gains[:, t : t + 1], scale=gains[t][:]
+                )
+            sin_sq = ring.tile([P, 4 * CH], F32, name="sin_sq")
+            nc.scalar.activation(sin_sq[:], half_sin[:], ACT.Square, scale=2.0)
+            z = ring.tile([P, 4 * CH], BF16, name="z", align_bytes=64)
+            nc.vector.scalar_tensor_tensor(
+                z[:].rearrange("p (j t) -> p j t", t=4), sin_sq[:].rearrange("p (j t) -> p j t", t=4), -2.0,
+                cos_gain[:].rearrange("p (t j) -> p j t", t=4), ALU.add, ALU.mult,
+            )
+            z_codes = ring.tile([P, CH], U32, name="z_codes", align_bytes=64)
+            z_scales = ring.tile([P, CH], U8, name="z_scales", align_bytes=64)
+            nc.vector.quantize_mx(out=z_codes[:].bitcast(E4M3), scales=z_scales[:], in_=z[:])
+            return z_codes, z_scales
+
+        def second_stage(zq, rows, name):
+            bank = psum.tile([P, len(rows) * CH], F32, name=name)
+            for u, n in enumerate(rows):
+                lhs, lhs_sc = e4m3_weight((w5_codes, w5_scales), n)
+                nc.tensor.matmul_mx(
+                    out=bank[:, u * CH : (u + 1) * CH], lhsT=lhs, lhsT_scale=lhs_sc,
+                    rhs=zq[0][:].bitcast(E4M3), rhs_scale=zq[1][:], start=True, stop=True,
+                )
+            return bank
+
+        def put(bank, rows, c, name):
+            y = ring.tile([P, len(rows) * CH], F32, name=name)
+            nc.scalar.copy(out=y[:], in_=bank[:])
+            for u, n in enumerate(rows):
+                nc.vector.tensor_tensor(
+                    pages[n][:].indirect(list3[:, c * CH // 16 : (c + 1) * CH // 16]),
+                    y[:, u * CH : (u + 1) * CH], wgo_sb[:, c * CH : (c + 1) * CH], ALU.mult,
+                )
+                if c == CHUNKS - 1:
+                    nc.sync.dma_start(out=out[n * P : (n + 1) * P, :], in_=pages[n][:])
+
+        late = None
+        for c in range(CHUNKS):
+            zq = first_stage(c)
+            if late is not None:
+                put(late, (2,), c - 1, "y_late")
+            put(second_stage(zq, (0, 1), "y_bank"), (0, 1), c, "y_early")
+            late = second_stage(zq, (2,), "y_bank_late")
+        put(late, (2,), CHUNKS - 1, "y_late")

@@ -20,6 +20,8 @@ ALU = mybir.AluOpType
 P = 128
 CH = 256
 CHUNKS = S // CH
+PS_BANKS = (0, 4, 2, 2)
+PC_BANKS = (2, 2, 2, 2)
 QUARTER_PI_HI = round(math.pi / 4 * 2**24) / 2**24
 QUARTER_PI_LO = math.pi / 4 - QUARTER_PI_HI
 
@@ -45,14 +47,11 @@ def tile_list_marker_slip_features_kernel(
         v_planes = held("v_planes", [P, 2 * S // 4], I32)
         fs_sc_raw = held("fs_sc_raw", [P, 2 * H // 4], I32)
         pc_sc_raw = held("pc_sc_raw", [P, H // 4], I32)
-        for zeroed in (tab_sc, tab2_sc, fs_sc_raw, pc_sc_raw, v_planes):
+        for zeroed in (tab_sc, tab2_sc):
+            nc.gpsimd.memset(zeroed[:, 0 : T // 8], 0)
+            nc.vector.memset(zeroed[:, T // 8 : T // 4], 0)
+        for zeroed in (v_planes, fs_sc_raw, pc_sc_raw):
             nc.vector.memset(zeroed[:], 0)
-
-        nc.sync.dma_start(list1[:], offs)
-        nc.sync.dma_start(out=tab_sc[0:P:4, :], in_=tab_scales.bitcast(I32).rearrange("a q w -> q a w"))
-        nc.sync.dma_start(list2[:], offs2)
-        for d in range(4):
-            nc.sync.dma_start(out=tab2_sc[32 * d : 32 * d + 4, :], in_=tab2_scales[0, 4 * d : 4 * d + 4, :].bitcast(I32))
 
         def load_weight(name, rows):
             raw = held(name, [P, 4 * H], F32)
@@ -64,32 +63,43 @@ def tile_list_marker_slip_features_kernel(
             nc.sync.dma_start(out=tile[:], in_=words.rearrange("p t i -> p (t i)").bitcast(I32))
             return tile
 
-        wps_raw = load_weight("wps_raw", wps)
-        wfc_raw = [load_weight("wfc_raw0", wfc[0:512, :])]
-        tab2_w = load_table("tab2_w", tab2_words[0])
-        fs_w_raw = held("fs_w_raw", [P, 2, H // 2], I32)
-        nc.sync.dma_start(out=fs_w_raw[:], in_=wfs_words.bitcast(I32).rearrange("a p w -> p a w"))
-        pc_w_raw = held("pc_w_raw", [P, H // 2], I32)
-        nc.sync.dma_start(out=pc_w_raw[:], in_=wpc_words[0].bitcast(I32))
-        for d in range(4):
-            nc.sync.dma_start(
-                out=fs_sc_raw[32 * d : 32 * d + 4, :],
-                in_=wfs_scales[:, 4 * d : 4 * d + 4, :].bitcast(I32).rearrange("a r w -> r a w"),
-            )
-        wfc_raw.append(load_weight("wfc_raw1", wfc[512:1024, :]))
-        for d in range(4):
-            nc.sync.dma_start(out=pc_sc_raw[32 * d : 32 * d + 4, :], in_=wpc_scales[0, 4 * d : 4 * d + 4, :].bitcast(I32))
-        tab_w = [load_table("tab_w0", tab_words[0]), load_table("tab_w1", tab_words[1])]
+        nc.sync.dma_start(list1[:], offs)
+        nc.sync.dma_start(list2[:], offs2)
         gains = [held("gain%d" % t, [P, 1], F32) for t in range(4)]
         with nc.allow_non_contiguous_dma(reason="one gain for each partition and slice"):
             for t in range(4):
                 nc.sync.dma_start(out=gains[t][:], in_=gain.rearrange("(q t i) -> t q i", t=4, i=8)[t])
+        nc.sync.dma_start(out=tab_sc[0:P:4, :], in_=tab_scales.bitcast(I32).rearrange("a q w -> q a w"))
+        tab2_w = load_table("tab2_w", tab2_words[0])
+        for r in range(4):
+            nc.sync.dma_start(out=tab2_sc[r:P:32, :], in_=tab2_scales[0, r:16:4, :].bitcast(I32))
+        wps_raw = load_weight("wps_raw", wps)
+        fs_w_raw = held("fs_w_raw", [P, 2, H // 2], I32)
+        nc.sync.dma_start(out=fs_w_raw[:], in_=wfs_words.bitcast(I32).rearrange("a p w -> p a w"))
+        pc_w_raw = held("pc_w_raw", [P, H // 2], I32)
+        nc.sync.dma_start(out=pc_w_raw[:], in_=wpc_words[0].bitcast(I32))
+        tab_w = [load_table("tab_w0", tab_words[0])]
+        v_sc_picked = held("v_sc_picked", [P, S], U8)
+        nc.vector.tensor_copy(v_sc_picked[:], tab_sc[:].bitcast(U8).indirect(list1[:]))
+        for d in range(4):
+            nc.sync.dma_start(out=v_planes[32 * d : 32 * d + 4, :], in_=v_sc_picked[32 * d : 32 * d + 32 : 4, :].bitcast(I32))
+        tab_w.append(load_table("tab_w1", tab_words[1]))
+        for r in range(4):
+            nc.sync.dma_start(out=fs_sc_raw[r:P:32, :], in_=wfs_scales[:, r:16:4, :].bitcast(I32).rearrange("a d w -> d a w"))
+        wfc0_raw = load_weight("wfc0_raw", wfc[0:512, :])
+        for r in range(4):
+            nc.sync.dma_start(out=pc_sc_raw[r:P:32, :], in_=wpc_scales[0, r:16:4, :].bitcast(I32))
+        wfc1_raw = []
+        for h in range(2):
+            raw = held("wfc1_raw%d" % h, [P, 4, H // 2], F32)
+            nc.sync.dma_start(out=raw[:], in_=wfc[512:1024, h * H // 2 : (h + 1) * H // 2].rearrange("(p j) c -> p j c", j=4))
+            wfc1_raw.append(raw)
+        nc.sync.dma_start(list3[:], offs3)
         w5_raw = held("w5_raw", [P, 4 * N], F32)
         for t in range(4):
             nc.sync.dma_start(out=w5_raw[:, t * N : (t + 1) * N], in_=w5.rearrange("(q t i) n -> t q i n", t=4, i=8)[t])
         wgo_sb = held("wgo_sb", [P, S], F32)
         nc.sync.dma_start(out=wgo_sb[:], in_=wgo)
-        nc.sync.dma_start(list3[:], offs3)
         pages = []
         for n in range(N // P):
             page = held("page%d" % n, [P, T2], F32)
@@ -98,19 +108,15 @@ def tile_list_marker_slip_features_kernel(
 
         ones = held("ones", [P, 1], F32)
         nc.vector.memset(ones[:], 1.0)
-        phase = held("phase", [P, 1], F32)
-        nc.vector.tensor_scalar(phase[:], ones[:], -QUARTER_PI_HI, -QUARTER_PI_LO, ALU.mult, ALU.add)
+        minus_quarter_pi = held("minus_quarter_pi", [P, 1], F32)
+        nc.vector.tensor_scalar(minus_quarter_pi[:], ones[:], -QUARTER_PI_HI, -QUARTER_PI_LO, ALU.mult, ALU.add)
+        half_pi = held("half_pi", [P, 1], F32)
+        nc.vector.tensor_scalar(half_pi[:], ones[:], 2 * QUARTER_PI_HI, 2 * QUARTER_PI_LO, ALU.mult, ALU.add)
 
-        v_sc_picked = held("v_sc_picked", [P, S], U8)
-        nc.vector.tensor_copy(v_sc_picked[:], tab_sc[:].bitcast(U8).indirect(list1[:]))
-        for d in range(4):
-            nc.gpsimd.dma_start(out=v_planes[32 * d : 32 * d + 4, :], in_=v_sc_picked[32 * d : 32 * d + 32 : 4, :].bitcast(I32))
-        v2_plane = held("v2_plane", [P, S], U8)
-        nc.vector.tensor_copy(v2_plane[:], tab2_sc[:].bitcast(U8).indirect(list2[:]))
         v_plane = v_planes[:].bitcast(U8)
 
         def round_weight(name, raw):
-            grouped = held(name, [P, 4 * H], BF16)
+            grouped = keep.tile([P, 4 * H], BF16, name=name, tag="wps_then_v0", align_bytes=64)
             nc.scalar.copy(
                 out=grouped[:].rearrange("p (t q i j) -> p q t i j", t=4, i=8, j=4),
                 in_=raw[:].rearrange("p (j q t i) -> p q t i j", j=4, t=4, i=8),
@@ -131,28 +137,23 @@ def tile_list_marker_slip_features_kernel(
             )
             return dealt[:].bitcast(U8)
 
-        def gather_words(name, table, offsets, c):
-            picked = held("%s_%d" % (name, c), [P, CH], U32)
-            nc.vector.tensor_copy(picked[:], table[:].bitcast(U32).indirect(offsets[:, c * CH // 16 : (c + 1) * CH // 16]))
-            return picked
+        def gather_words(picked, table, offsets, chunks):
+            parts = {}
+            for u, c in enumerate(chunks):
+                parts[c] = picked[:, u * CH : (u + 1) * CH]
+                nc.vector.tensor_copy(parts[c], table[:].bitcast(U32).indirect(offsets[:, c * CH // 16 : (c + 1) * CH // 16]))
+            return parts
 
-        wps_q = quantise("wps", round_weight("wps_bf", wps_raw), H)
-        v2 = [gather_words("v2", tab2_w, list2, c) for c in range(CHUNKS)]
-        wfc_q = [quantise("wfc0", round_weight("wfc0_bf", wfc_raw[0]), H)]
+        wps_bf = round_weight("wps_bf", wps_raw)
+        v2 = gather_words(held("v2", [P, S], U32), tab2_w, list2, range(CHUNKS))
+        v2_plane = held("v2_plane", [P, S], U8)
+        nc.vector.tensor_copy(v2_plane[:], tab2_sc[:].bitcast(U8).indirect(list2[:]))
+        wps_q = quantise("wps", wps_bf, H)
         fs_w = deal("fs_w", fs_w_raw[:].rearrange("p a w -> p (a w)"), 2, 4)
         pc_w = deal("pc_w", pc_w_raw[:], 1, 4)
         fs_sc = deal("fs_sc", fs_sc_raw[:], 2, 2)
-        pc_sc = deal("pc_sc", pc_sc_raw[:], 1, 2)
-        wfc_q.append(quantise("wfc1", round_weight("wfc1_bf", wfc_raw[1]), H))
-        v = [[gather_words("v%d" % a, tab_w[a], list1, c) for c in range(CHUNKS)] for a in range(2)]
-        half_gains = held("half_gains", [P, 4], F32)
-        for t in range(4):
-            nc.vector.tensor_scalar(half_gains[:, t : t + 1], gains[t][:], -0.5, None, ALU.mult)
-        w5_bf = held("w5_bf", [P, 4 * N], BF16)
-        nc.vector.tensor_copy(
-            out=w5_bf[:].rearrange("p (n t) -> p n t", t=4), in_=w5_raw[:].rearrange("p (t n) -> p n t", t=4)
-        )
-        w5_codes, w5_scales = quantise("w5", w5_bf, N)
+        v0 = keep.tile([P, S], U32, name="v0", tag="wps_then_v0", align_bytes=64)
+        v = [gather_words(v0, tab_w[0], list1, range(CHUNKS)), gather_words(held("v1", [P, 2 * CH], U32), tab_w[1], list1, range(2))]
 
         def e4m3_weight(q, t):
             return q[0][:, t * P : (t + 1) * P].bitcast(E4M3), q[1][:, t * P : (t + 1) * P]
@@ -162,8 +163,8 @@ def tile_list_marker_slip_features_kernel(
             return words[:, 2 * c0 : 2 * (c0 + P)].bitcast(E2M1), scales[:, c0 : c0 + P]
 
         def moving(k, c, j0, width):
-            cols = slice(j0, j0 + width)
             g0 = c * CH + j0
+            cols = slice(j0, j0 + width)
             if k == 0:
                 return v2[c][:, cols].bitcast(E4M3), v2_plane[:, g0 : g0 + width]
             a = k - 1
@@ -185,66 +186,135 @@ def tile_list_marker_slip_features_kernel(
                     start=(k, u, t) == steps[0], stop=(k, u, t) == steps[-1],
                 )
 
-        def first_stage(c):
-            half_cos = ring.tile([P, 4 * CH], F32, name="half_cos")
+        z_codes = held("z_codes", [P, S], U32)
+        z_scales = held("z_scales", [P, S], U8)
+
+        def phase_bank(first, weight, c, h):
+            bank = psum.tile([P, 2 * CH], F32, name="phase_bank", tag="bank%d" % (first + h))
+            phase_sums(bank, weight, (2 * h, 2 * h + 1), c, 0, CH)
+            return bank
+
+        def half_sines(c):
+            half_sin = ring.tile([P, 4 * CH], F32, name="half_sin", bufs=1)
             for h in range(2):
-                bank = psum.tile([P, 2 * CH], F32, name="pc_bank", bufs=3)
-                phase_sums(bank, pc_weight, (2 * h, 2 * h + 1), c, 0, CH)
-                nc.scalar.activation(half_cos[:, 2 * h * CH : 2 * (h + 1) * CH], bank[:], ACT.Sin, scale=0.5)
-            half_sin = ring.tile([P, 4 * CH], F32, name="half_sin")
-            for h in range(2):
-                bank = psum.tile([P, 4 * P], F32, name="ps_bank", bufs=3)
-                phase_sums(bank, ps_weight, (0, 1, 2, 3), c, h * P, P)
+                bank = phase_bank(PS_BANKS[c], ps_weight, c, h)
                 nc.scalar.activation(
-                    half_sin[:, 4 * h * P : 4 * (h + 1) * P].rearrange("p (j t) -> p j t", t=4),
-                    bank[:].rearrange("p (t j) -> p j t", t=4), ACT.Sin, bias=phase[:], scale=0.5,
+                    half_sin[:, 2 * h * CH : 2 * (h + 1) * CH], bank[:], ACT.Sin, bias=minus_quarter_pi[:], scale=0.5
                 )
-            cos_sq = ring.tile([P, 4 * CH], F32, name="cos_sq")
-            nc.scalar.activation(cos_sq[:], half_cos[:], ACT.Square)
-            cos_gain = ring.tile([P, 4 * CH], F32, name="cos_gain")
+            return half_sin
+
+        def gained_sine(half_sin):
+            sin_sq = ring.tile([P, 4 * CH], F32, name="sin_sq", bufs=1)
+            nc.scalar.activation(sin_sq[:], half_sin[:], ACT.Square)
+            sine = ring.tile([P, 4 * CH], F32, name="sine")
             for t in range(4):
                 cols = slice(t * CH, (t + 1) * CH)
                 nc.scalar.activation(
-                    cos_gain[:, cols], cos_sq[:, cols], ACT.Identity, bias=half_gains[:, t : t + 1], scale=gains[t][:]
+                    sine[:, cols], sin_sq[:, cols], ACT.Identity, bias=gains[t][:], scale=slopes[:, t : t + 1]
                 )
-            sin_sq = ring.tile([P, 4 * CH], F32, name="sin_sq")
-            nc.scalar.activation(sin_sq[:], half_sin[:], ACT.Square, scale=2.0)
-            z = ring.tile([P, 4 * CH], BF16, name="z", align_bytes=64)
-            nc.vector.scalar_tensor_tensor(
-                z[:].rearrange("p (j t) -> p j t", t=4), sin_sq[:].rearrange("p (j t) -> p j t", t=4), -2.0,
-                cos_gain[:].rearrange("p (t j) -> p j t", t=4), ALU.add, ALU.mult,
-            )
-            z_codes = ring.tile([P, CH], U32, name="z_codes", align_bytes=64)
-            z_scales = ring.tile([P, CH], U8, name="z_scales", align_bytes=64)
-            nc.vector.quantize_mx(out=z_codes[:].bitcast(E4M3), scales=z_scales[:], in_=z[:])
-            return z_codes, z_scales
+            return sine
 
-        def second_stage(zq, rows, name):
-            bank = psum.tile([P, len(rows) * CH], F32, name=name)
+        def gained_sine_on_vector(half_sin):
+            sin_sq = keep.tile([P, 4 * CH], F32, name="sin_sq1", tag="cosine0", align_bytes=64)
+            nc.vector.tensor_tensor(sin_sq[:], half_sin[:], half_sin[:], ALU.mult)
+            sine = ring.tile([P, 4 * CH], F32, name="sine")
+            for t in range(4):
+                cols = slice(t * CH, (t + 1) * CH)
+                nc.vector.tensor_scalar(sine[:, cols], sin_sq[:, cols], slopes[:, t : t + 1], gains[t][:], ALU.mult, ALU.add)
+            return sine
+
+        def magnitudes(c):
+            size = keep.tile([P, 4 * CH], F32, name="size", tag="size%d" % c)
+            for h in range(2):
+                bank = phase_bank(PC_BANKS[c], pc_weight, c, h)
+                nc.scalar.activation(size[:, 2 * h * CH : 2 * (h + 1) * CH], bank[:], ACT.Abs)
+            return size
+
+        def features(c, size, sine):
+            cosine = keep.tile([P, 4 * CH], F32, name="cosine", tag="cosine%d" % min(c, 1), align_bytes=64)
+            nc.scalar.activation(cosine[:], size[:], ACT.Sin, bias=half_pi[:], scale=-1.0)
+            z = ring.tile([P, 4 * CH], BF16, name="z", align_bytes=64)
+            nc.vector.tensor_tensor(
+                z[:].rearrange("p (g i t) -> p g t i", i=4, t=4),
+                cosine[:].rearrange("p (t g i) -> p g t i", i=4, t=4),
+                sine[:].rearrange("p (t g i) -> p g t i", i=4, t=4), ALU.mult,
+            )
+            cols = slice(c * CH, (c + 1) * CH)
+            nc.vector.quantize_mx(out=z_codes[:, cols].bitcast(E4M3), scales=z_scales[:, cols], in_=z[:])
+
+        def put(rows, j0, width, which, y):
+            cols = slice(j0, j0 + width)
+            bank = psum.tile([P, 512], F32, name="y_bank", tag="bank%d" % which)
             for u, n in enumerate(rows):
                 lhs, lhs_sc = e4m3_weight((w5_codes, w5_scales), n)
                 nc.tensor.matmul_mx(
-                    out=bank[:, u * CH : (u + 1) * CH], lhsT=lhs, lhsT_scale=lhs_sc,
-                    rhs=zq[0][:].bitcast(E4M3), rhs_scale=zq[1][:], start=True, stop=True,
+                    out=bank[:, u * width : (u + 1) * width], lhsT=lhs, lhsT_scale=lhs_sc,
+                    rhs=z_codes[:, cols].bitcast(E4M3), rhs_scale=z_scales[:, cols], start=True, stop=True,
                 )
-            return bank
-
-        def put(bank, rows, c, name):
-            y = ring.tile([P, len(rows) * CH], F32, name=name)
-            nc.scalar.copy(out=y[:], in_=bank[:])
+            used = len(rows) * width
+            nc.scalar.copy(out=y[:, 0:used], in_=bank[:, 0:used])
             for u, n in enumerate(rows):
                 nc.vector.tensor_tensor(
-                    pages[n][:].indirect(list3[:, c * CH // 16 : (c + 1) * CH // 16]),
-                    y[:, u * CH : (u + 1) * CH], wgo_sb[:, c * CH : (c + 1) * CH], ALU.mult,
+                    pages[n][:].indirect(list3[:, j0 // 16 : (j0 + width) // 16]),
+                    y[:, u * width : (u + 1) * width], wgo_sb[:, cols], ALU.mult,
                 )
-                if c == CHUNKS - 1:
+                if j0 + width == S:
                     nc.sync.dma_start(out=out[n * P : (n + 1) * P, :], in_=pages[n][:])
 
-        late = None
-        for c in range(CHUNKS):
-            zq = first_stage(c)
-            if late is not None:
-                put(late, (2,), c - 1, "y_late")
-            put(second_stage(zq, (0, 1), "y_bank"), (0, 1), c, "y_early")
-            late = second_stage(zq, (2,), "y_bank_late")
-        put(late, (2,), CHUNKS - 1, "y_late")
+        slopes = held("slopes", [P, 4], F32)
+        for t in range(4):
+            nc.vector.tensor_scalar(slopes[:, t : t + 1], gains[t][:], -2.0, None, ALU.mult)
+        sine0 = gained_sine(half_sines(0))
+        half_sin1 = half_sines(1)
+        wfc0_bf = held("wfc0_bf", [P, 4 * H], BF16)
+        dst = wfc0_bf[:].rearrange("p (t q i j) -> p q t i j", t=4, i=8, j=4)
+        src = wfc0_raw[:].rearrange("p (j q t i) -> p q t i j", j=4, t=4, i=8)
+        nc.vector.tensor_copy(out=dst, in_=src)
+        pc_sc_dealt = held("pc_sc", [P, H // 4], I32)
+        nc.vector.tensor_copy(
+            out=pc_sc_dealt[:].rearrange("p (t q w) -> p t q w", t=4, w=2),
+            in_=pc_sc_raw[:].rearrange("p (q t w) -> p t q w", t=4, w=2),
+        )
+        pc_sc = pc_sc_dealt[:].bitcast(U8)
+        wfc_q = [quantise("wfc0", wfc0_bf, H)]
+        wfc1_bf = keep.tile([P, 4 * H], BF16, name="wfc1_bf", tag="wfc1_bf", align_bytes=64)
+        dst = wfc1_bf[:].rearrange("p (t q i j) -> p q t i j", t=4, i=8, j=4)
+        for h in range(2):
+            nc.vector.tensor_copy(
+                out=dst[:, 8 * h : 8 * (h + 1)], in_=wfc1_raw[h][:].rearrange("p j (q t i) -> p q t i j", t=4, i=8)
+            )
+        wfc1_codes = held("wfc1_codes", [P, H], U32)
+        wfc1_scales = held("wfc1_scales", [P, H], U8)
+        for h in range(2):
+            cols = slice(h * H // 2, (h + 1) * H // 2)
+            nc.vector.quantize_mx(
+                out=wfc1_codes[:, cols].bitcast(E4M3), scales=wfc1_scales[:, cols], in_=wfc1_bf[:, 2 * h * H : 2 * (h + 1) * H]
+            )
+        wfc_q.append((wfc1_codes, wfc1_scales))
+        w5_bf = held("w5_bf", [P, 4 * N], BF16)
+        nc.vector.tensor_copy(
+            out=w5_bf[:].rearrange("p (g i t) -> p g t i", i=4, t=4),
+            in_=w5_raw[:].rearrange("p (t g i) -> p g t i", i=4, t=4),
+        )
+        w5_codes, w5_scales = quantise("w5", w5_bf, N)
+
+        late = keep.tile([P, 2 * CH], U32, name="late", tag="wfc1_bf", align_bytes=64)
+        v[1] = {**v[1], **gather_words(late, tab_w[1], list1, (2, 3))}
+        features(0, magnitudes(0), sine0)
+        sine1 = gained_sine_on_vector(half_sin1)
+        put((0, 1), 0, CH, 6, held("y_first", [P, 2 * CH], F32))
+        features(1, magnitudes(1), sine1)
+        put((2,), 0, CH, 7, keep.tile([P, CH], F32, name="y0", tag="size1"))
+        sine = gained_sine(half_sines(2))
+        size = magnitudes(2)
+        put((0,), CH, CH, 2, held("y1a", [P, CH], F32))
+        features(2, size, sine)
+        put((1, 2), CH, CH, 0, keep.tile([P, 2 * CH], F32, name="y1b", tag="size2"))
+        sine = gained_sine(half_sines(3))
+        size = magnitudes(3)
+        put((0,), 2 * CH, CH, 2, held("y2a", [P, CH], F32))
+        features(3, size, sine)
+        put((1,), 2 * CH, CH, 1, keep.tile([P, CH], F32, name="y2b", tag="size3"))
+        put((0,), 3 * CH, CH, 4, held("y3a", [P, CH], F32))
+        put((1,), 3 * CH, CH, 6, held("y3b", [P, CH], F32))
+        put((2,), 2 * CH, 2 * CH, 5, held("y4", [P, 2 * CH], F32))

@@ -137,15 +137,15 @@ def tile_list_marker_slip_features_kernel(
             )
             return dealt[:].bitcast(U8)
 
-        def gather_words(picked, table, offsets, chunks):
-            parts = {}
-            for u, c in enumerate(chunks):
-                parts[c] = picked[:, u * CH : (u + 1) * CH]
-                nc.vector.tensor_copy(parts[c], table[:].bitcast(U32).indirect(offsets[:, c * CH // 16 : (c + 1) * CH // 16]))
-            return parts
+        def gather_words(picked, table, offsets, first, count):
+            nc.vector.tensor_copy(
+                picked[:, 0 : count * CH],
+                table[:].bitcast(U32).indirect(offsets[:, first * CH // 16 : (first + count) * CH // 16]),
+            )
+            return [picked[:, u * CH : (u + 1) * CH] for u in range(count)]
 
         wps_bf = round_weight("wps_bf", wps_raw)
-        v2 = gather_words(held("v2", [P, S], U32), tab2_w, list2, range(CHUNKS))
+        v2 = gather_words(held("v2", [P, S], U32), tab2_w, list2, 0, CHUNKS)
         v2_plane = held("v2_plane", [P, S], U8)
         nc.vector.tensor_copy(v2_plane[:], tab2_sc[:].bitcast(U8).indirect(list2[:]))
         wps_q = quantise("wps", wps_bf, H)
@@ -153,7 +153,9 @@ def tile_list_marker_slip_features_kernel(
         pc_w = deal("pc_w", pc_w_raw[:], 1, 4)
         fs_sc = deal("fs_sc", fs_sc_raw[:], 2, 2)
         v0 = keep.tile([P, S], U32, name="v0", tag="wps_then_v0", align_bytes=64)
-        v = [gather_words(v0, tab_w[0], list1, range(CHUNKS)), gather_words(held("v1", [P, 2 * CH], U32), tab_w[1], list1, range(2))]
+        v = [gather_words(v0, tab_w[0], list1, 0, CHUNKS)]
+        early = held("early", [P, 2 * CH], U32)
+        v.append([gather_words(early[:, c * CH : (c + 1) * CH], tab_w[1], list1, c, 1)[0] for c in range(2)])
 
         def e4m3_weight(q, t):
             return q[0][:, t * P : (t + 1) * P].bitcast(E4M3), q[1][:, t * P : (t + 1) * P]
@@ -263,7 +265,7 @@ def tile_list_marker_slip_features_kernel(
 
         slopes = held("slopes", [P, 4], F32)
         for t in range(4):
-            nc.vector.tensor_scalar(slopes[:, t : t + 1], gains[t][:], -2.0, None, ALU.mult)
+            nc.scalar.activation(slopes[:, t : t + 1], gains[t][:], ACT.Copy, scale=-2.0)
         sine0 = gained_sine(half_sines(0))
         half_sin1 = half_sines(1)
         wfc0_bf = held("wfc0_bf", [P, 4 * H], BF16)
@@ -299,7 +301,7 @@ def tile_list_marker_slip_features_kernel(
         w5_codes, w5_scales = quantise("w5", w5_bf, N)
 
         late = keep.tile([P, 2 * CH], U32, name="late", tag="wfc1_bf", align_bytes=64)
-        v[1] = {**v[1], **gather_words(late, tab_w[1], list1, (2, 3))}
+        v[1].extend([gather_words(late[:, u * CH : (u + 1) * CH], tab_w[1], list1, 2 + u, 1)[0] for u in range(2)])
         features(0, magnitudes(0), sine0)
         sine1 = gained_sine_on_vector(half_sin1)
         put((0, 1), 0, CH, 6, held("y_first", [P, 2 * CH], F32))

import math
from contextlib import ExitStack

import concourse.mybir as mybir

K, M, H, N, T, S, T2 = 1024, 512, 512, 384, 2048, 1024, 2048
FLOPS = 2 * S * H * (2 * K + 2 * M) + 2 * S * H * N

F32 = mybir.dt.float32
BF16 = mybir.dt.bfloat16
I32 = mybir.dt.int32
U32 = mybir.dt.uint32
U16 = mybir.dt.uint16
U8 = mybir.dt.uint8
E4M3 = mybir.dt.float8_e4m3fn_x4
E2M1 = mybir.dt.float4_e2m1fn_x4
ACT = mybir.ActivationFunctionType
ALU = mybir.AluOpType

P = 128
CH = 256
CHUNKS = S // CH
PS_BANKS = (0, 4, 2, 2)
PC_BANKS = (2, 2, 2, 2)
QUARTER_PI_HI = round(math.pi / 4 * 2**24) / 2**24
QUARTER_PI_LO = math.pi / 4 - QUARTER_PI_HI


def tile_list_marker_slip_features_kernel(
    tc, tab_words, tab_scales, tab2_words, tab2_scales, offs, offs2, offs3, wfc, wpc_words, wpc_scales,
    wfs_words, wfs_scales, wps, gain, w5, wgo, page1, out,
):
    nc = tc.nc
    with ExitStack() as ctx:
        keep = ctx.enter_context(tc.tile_pool(name="keep", bufs=1))
        ring = ctx.enter_context(tc.tile_pool(name="ring", bufs=2))
        psum = ctx.enter_context(tc.psum_pool(name="psum", bufs=1))

        def held(name, shape, dtype):
            return keep.tile(shape, dtype, name=name, align_bytes=64)

        list1 = held("list1", [P, S // 16], U16)
        list2 = held("list2", [P, S // 16], U16)
        list3 = held("list3", [P, S // 16], U16)
        tab_sc = held("tab_sc", [P, T // 4], I32)
        tab2_sc = held("tab2_sc", [P, T // 4], I32)
        v_planes = held("v_planes", [P, 2 * S // 4], I32)
        fs_sc_raw = held("fs_sc_raw", [P, 2 * H // 4], I32)
        pc_sc_raw = held("pc_sc_raw", [P, H // 4], I32)
        for zeroed in (tab_sc, tab2_sc):
            nc.gpsimd.memset(zeroed[:, 0 : T // 8], 0)
            nc.vector.memset(zeroed[:, T // 8 : T // 4], 0)
        for zeroed in (v_planes, fs_sc_raw, pc_sc_raw):
            nc.vector.memset(zeroed[:], 0)

        def load_weight(name, rows):
            raw = held(name, [P, 4 * H], F32)
            nc.sync.dma_start(out=raw[:], in_=rows.rearrange("(p j) c -> p (j c)", j=4))
            return raw

        def load_table(name, words):
            tile = held(name, [P, T], I32)
            nc.sync.dma_start(out=tile[:], in_=words.rearrange("p t i -> p (t i)").bitcast(I32))
            return tile

        nc.sync.dma_start(list1[:], offs)
        nc.sync.dma_start(list2[:], offs2)
        gains = [held("gain%d" % t, [P, 1], F32) for t in range(4)]
        with nc.allow_non_contiguous_dma(reason="one gain for each partition and slice"):
            for t in range(4):
                nc.sync.dma_start(out=gains[t][:], in_=gain.rearrange("(q t i) -> t q i", t=4, i=8)[t])
        nc.sync.dma_start(out=tab_sc[0:P:4, :], in_=tab_scales.bitcast(I32).rearrange("a q w -> q a w"))
        tab2_w = load_table("tab2_w", tab2_words[0])
        for r in range(4):
            nc.sync.dma_start(out=tab2_sc[r:P:32, :], in_=tab2_scales[0, r:16:4, :].bitcast(I32))
        wps_raw = load_weight("wps_raw", wps)
        fs_w_raw = held("fs_w_raw", [P, 2, H // 2], I32)
        nc.sync.dma_start(out=fs_w_raw[:], in_=wfs_words.bitcast(I32).rearrange("a p w -> p a w"))
        pc_w_raw = held("pc_w_raw", [P, H // 2], I32)
        nc.sync.dma_start(out=pc_w_raw[:], in_=wpc_words[0].bitcast(I32))
        tab_w = [load_table("tab_w0", tab_words[0])]
        v_sc_picked = held("v_sc_picked", [P, S], U8)
        nc.vector.tensor_copy(v_sc_picked[:], tab_sc[:].bitcast(U8).indirect(list1[:]))
        for d in range(4):
            nc.sync.dma_start(out=v_planes[32 * d : 32 * d + 4, :], in_=v_sc_picked[32 * d : 32 * d + 32 : 4, :].bitcast(I32))
        tab_w.append(load_table("tab_w1", tab_words[1]))
        for r in range(4):
            nc.sync.dma_start(out=fs_sc_raw[r:P:32, :], in_=wfs_scales[:, r:16:4, :].bitcast(I32).rearrange("a d w -> d a w"))
        wfc0_raw = load_weight("wfc0_raw", wfc[0:512, :])
        for r in range(4):
            nc.sync.dma_start(out=pc_sc_raw[r:P:32, :], in_=wpc_scales[0, r:16:4, :].bitcast(I32))
        wfc1_raw = []
        for h in range(2):
            raw = held("wfc1_raw%d" % h, [P, 4, H // 2], F32)
            nc.sync.dma_start(out=raw[:], in_=wfc[512:1024, h * H // 2 : (h + 1) * H // 2].rearrange("(p j) c -> p j c", j=4))
            wfc1_raw.append(raw)
        nc.sync.dma_start(list3[:], offs3)
        w5_raw = held("w5_raw", [P, 4 * N], F32)
        for t in range(4):
            nc.sync.dma_start(out=w5_raw[:, t * N : (t + 1) * N], in_=w5.rearrange("(q t i) n -> t q i n", t=4, i=8)[t])
        wgo_sb = held("wgo_sb", [P, S], F32)
        nc.sync.dma_start(out=wgo_sb[:], in_=wgo)
        pages = []
        for n in range(N // P):
            page = held("page%d" % n, [P, T2], F32)
            nc.sync.dma_start(out=page[:], in_=page1[n * P : (n + 1) * P, :])
            pages.append(page)

        ones = held("ones", [P, 1], F32)
        nc.vector.memset(ones[:], 1.0)
        minus_quarter_pi = held("minus_quarter_pi", [P, 1], F32)
        nc.vector.tensor_scalar(minus_quarter_pi[:], ones[:], -QUARTER_PI_HI, -QUARTER_PI_LO, ALU.mult, ALU.add)
        half_pi = held("half_pi", [P, 1], F32)
        nc.vector.tensor_scalar(half_pi[:], ones[:], 2 * QUARTER_PI_HI, 2 * QUARTER_PI_LO, ALU.mult, ALU.add)

        v_plane = v_planes[:].bitcast(U8)

        def round_weight(name, raw):
            grouped = keep.tile([P, 4 * H], BF16, name=name, tag="wps_then_v0", align_bytes=64)
            nc.scalar.copy(
                out=grouped[:].rearrange("p (t q i j) -> p q t i j", t=4, i=8, j=4),
                in_=raw[:].rearrange("p (j q t i) -> p q t i j", j=4, t=4, i=8),
            )
            return grouped

        def quantise(name, grouped, width):
            codes = held(name + "_codes", [P, width], U32)
            scales = held(name + "_scales", [P, width], U8)
            nc.vector.quantize_mx(out=codes[:].bitcast(E4M3), scales=scales[:], in_=grouped[:])
            return codes, scales

        def deal(name, raw, passes, run):
            dealt = held(name, [P, passes * 64 * run], U32)
            nc.scalar.copy(
                out=dealt[:].rearrange("p (a t q w) -> p a t q w", a=passes, t=4, w=run),
                in_=raw.bitcast(U32).rearrange("p (a q t w) -> p a t q w", a=passes, t=4, w=run),
            )
            return dealt[:].bitcast(U8)

        def gather_words(picked, table, offsets, first, count):
            nc.vector.tensor_copy(
                picked[:, 0 : count * CH],
                table[:].bitcast(U32).indirect(offsets[:, first * CH // 16 : (first + count) * CH // 16]),
            )
            return [picked[:, u * CH : (u + 1) * CH] for u in range(count)]

        wps_bf = round_weight("wps_bf", wps_raw)
        v2 = gather_words(held("v2", [P, S], U32), tab2_w, list2, 0, CHUNKS)
        v2_plane = held("v2_plane", [P, S], U8)
        nc.vector.tensor_copy(v2_plane[:], tab2_sc[:].bitcast(U8).indirect(list2[:]))
        wps_q = quantise("wps", wps_bf, H)
        fs_w = deal("fs_w", fs_w_raw[:].rearrange("p a w -> p (a w)"), 2, 4)
        pc_w = deal("pc_w", pc_w_raw[:], 1, 4)
        fs_sc = deal("fs_sc", fs_sc_raw[:], 2, 2)
        v0 = keep.tile([P, S], U32, name="v0", tag="wps_then_v0", align_bytes=64)
        v = [gather_words(v0, tab_w[0], list1, 0, CHUNKS)]
        early = held("early", [P, 2 * CH], U32)
        v.append([gather_words(early[:, c * CH : (c + 1) * CH], tab_w[1], list1, c, 1)[0] for c in range(2)])

        def e4m3_weight(q, t):
            return q[0][:, t * P : (t + 1) * P].bitcast(E4M3), q[1][:, t * P : (t + 1) * P]

        def e2m1_weight(words, scales, a, t):
            c0 = a * H + t * P
            return words[:, 2 * c0 : 2 * (c0 + P)].bitcast(E2M1), scales[:, c0 : c0 + P]

        def moving(k, c, j0, width):
            g0 = c * CH + j0
            cols = slice(j0, j0 + width)
            if k == 0:
                return v2[c][:, cols].bitcast(E4M3), v2_plane[:, g0 : g0 + width]
            a = k - 1
            return v[a][c][:, cols].bitcast(E4M3), v_plane[:, a * S + g0 : a * S + g0 + width]

        def pc_weight(k, t):
            return e2m1_weight(pc_w, pc_sc, 0, t) if k == 0 else e4m3_weight(wfc_q[k - 1], t)

        def ps_weight(k, t):
            return e4m3_weight(wps_q, t) if k == 0 else e2m1_weight(fs_w, fs_sc, k - 1, t)

        def phase_sums(bank, weight, slices, c, j0, width):
            steps = [(k, u, t) for k in range(3) for u, t in enumerate(slices)]
            for k, u, t in steps:
                lhs, lhs_sc = weight(k, t)
                rhs, rhs_sc = moving(k, c, j0, width)
                nc.tensor.matmul_mx(
                    out=bank[:, u * width : (u + 1) * width], lhsT=lhs, lhsT_scale=lhs_sc, rhs=rhs, rhs_scale=rhs_sc,
                    start=(k, u, t) == steps[0], stop=(k, u, t) == steps[-1],
                )

        z_codes = held("z_codes", [P, S], U32)
        z_scales = held("z_scales", [P, S], U8)

        def phase_bank(first, weight, c, h):
            bank = psum.tile([P, 2 * CH], F32, name="phase_bank", tag="bank%d" % (first + h))
            phase_sums(bank, weight, (2 * h, 2 * h + 1), c, 0, CH)
            return bank

        def half_sines(c):
            half_sin = ring.tile([P, 4 * CH], F32, name="half_sin", bufs=1)
            for h in range(2):
                bank = phase_bank(PS_BANKS[c], ps_weight, c, h)
                nc.scalar.activation(
                    half_sin[:, 2 * h * CH : 2 * (h + 1) * CH], bank[:], ACT.Sin, bias=minus_quarter_pi[:], scale=0.5
                )
            return half_sin

        def gained_sine(half_sin):
            sin_sq = ring.tile([P, 4 * CH], F32, name="sin_sq", bufs=1)
            nc.scalar.activation(sin_sq[:], half_sin[:], ACT.Square)
            sine = ring.tile([P, 4 * CH], F32, name="sine")
            for t in range(4):
                cols = slice(t * CH, (t + 1) * CH)
                nc.scalar.activation(
                    sine[:, cols], sin_sq[:, cols], ACT.Identity, bias=gains[t][:], scale=slopes[:, t : t + 1]
                )
            return sine

        def gained_sine_on_vector(half_sin):
            sin_sq = keep.tile([P, 4 * CH], F32, name="sin_sq1", tag="cosine0", align_bytes=64)
            nc.vector.tensor_tensor(sin_sq[:], half_sin[:], half_sin[:], ALU.mult)
            sine = ring.tile([P, 4 * CH], F32, name="sine")
            for t in range(4):
                cols = slice(t * CH, (t + 1) * CH)
                nc.vector.tensor_scalar(sine[:, cols], sin_sq[:, cols], slopes[:, t : t + 1], gains[t][:], ALU.mult, ALU.add)
            return sine

        def magnitudes(c):
            size = keep.tile([P, 4 * CH], F32, name="size", tag="size%d" % c)
            for h in range(2):
                bank = phase_bank(PC_BANKS[c], pc_weight, c, h)
                nc.scalar.activation(size[:, 2 * h * CH : 2 * (h + 1) * CH], bank[:], ACT.Abs)
            return size

        def features(c, size, sine):
            cosine = keep.tile([P, 4 * CH], F32, name="cosine", tag="cosine%d" % min(c, 1), align_bytes=64)
            nc.scalar.activation(cosine[:], size[:], ACT.Sin, bias=half_pi[:], scale=-1.0)
            z = ring.tile([P, 4 * CH], BF16, name="z", align_bytes=64)
            nc.vector.tensor_tensor(
                z[:].rearrange("p (g i t) -> p g t i", i=4, t=4),
                cosine[:].rearrange("p (t g i) -> p g t i", i=4, t=4),
                sine[:].rearrange("p (t g i) -> p g t i", i=4, t=4), ALU.mult,
            )
            cols = slice(c * CH, (c + 1) * CH)
            nc.vector.quantize_mx(out=z_codes[:, cols].bitcast(E4M3), scales=z_scales[:, cols], in_=z[:])

        def put(rows, j0, width, which, y):
            cols = slice(j0, j0 + width)
            bank = psum.tile([P, 512], F32, name="y_bank", tag="bank%d" % which)
            for u, n in enumerate(rows):
                lhs, lhs_sc = e4m3_weight((w5_codes, w5_scales), n)
                nc.tensor.matmul_mx(
                    out=bank[:, u * width : (u + 1) * width], lhsT=lhs, lhsT_scale=lhs_sc,
                    rhs=z_codes[:, cols].bitcast(E4M3), rhs_scale=z_scales[:, cols], start=True, stop=True,
                )
            used = len(rows) * width
            nc.scalar.copy(out=y[:, 0:used], in_=bank[:, 0:used])
            for u, n in enumerate(rows):
                nc.vector.tensor_tensor(
                    pages[n][:].indirect(list3[:, j0 // 16 : (j0 + width) // 16]),
                    y[:, u * width : (u + 1) * width], wgo_sb[:, cols], ALU.mult,
                )
                if j0 + width == S:
                    nc.sync.dma_start(out=out[n * P : (n + 1) * P, :], in_=pages[n][:])

        slopes = held("slopes", [P, 4], F32)
        for t in range(4):
            nc.scalar.activation(slopes[:, t : t + 1], gains[t][:], ACT.Copy, scale=-2.0)
        sine0 = gained_sine(half_sines(0))
        half_sin1 = half_sines(1)
        wfc0_bf = held("wfc0_bf", [P, 4 * H], BF16)
        dst = wfc0_bf[:].rearrange("p (t q i j) -> p q t i j", t=4, i=8, j=4)
        src = wfc0_raw[:].rearrange("p (j q t i) -> p q t i j", j=4, t=4, i=8)
        nc.vector.tensor_copy(out=dst, in_=src)
        pc_sc_dealt = held("pc_sc", [P, H // 4], I32)
        nc.vector.tensor_copy(
            out=pc_sc_dealt[:].rearrange("p (t q w) -> p t q w", t=4, w=2),
            in_=pc_sc_raw[:].rearrange("p (q t w) -> p t q w", t=4, w=2),
        )
        pc_sc = pc_sc_dealt[:].bitcast(U8)
        wfc_q = [quantise("wfc0", wfc0_bf, H)]
        wfc1_bf = keep.tile([P, 4 * H], BF16, name="wfc1_bf", tag="wfc1_bf", align_bytes=64)
        dst = wfc1_bf[:].rearrange("p (t q i j) -> p q t i j", t=4, i=8, j=4)
        for h in range(2):
            nc.vector.tensor_copy(
                out=dst[:, 8 * h : 8 * (h + 1)], in_=wfc1_raw[h][:].rearrange("p j (q t i) -> p q t i j", t=4, i=8)
            )
        wfc1_codes = held("wfc1_codes", [P, H], U32)
        wfc1_scales = held("wfc1_scales", [P, H], U8)
        for h in range(2):
            cols = slice(h * H // 2, (h + 1) * H // 2)
            nc.vector.quantize_mx(
                out=wfc1_codes[:, cols].bitcast(E4M3), scales=wfc1_scales[:, cols], in_=wfc1_bf[:, 2 * h * H : 2 * (h + 1) * H]
            )
        wfc_q.append((wfc1_codes, wfc1_scales))
        w5_bf = held("w5_bf", [P, 4 * N], BF16)
        nc.vector.tensor_copy(
            out=w5_bf[:].rearrange("p (g i t) -> p g t i", i=4, t=4),
            in_=w5_raw[:].rearrange("p (t g i) -> p g t i", i=4, t=4),
        )
        w5_codes, w5_scales = quantise("w5", w5_bf, N)

        late = keep.tile([P, 2 * CH], U32, name="late", tag="wfc1_bf", align_bytes=64)
        v[1].extend([gather_words(late[:, u * CH : (u + 1) * CH], tab_w[1], list1, 2 + u, 1)[0] for u in range(2)])
        features(0, magnitudes(0), sine0)
        sine1 = gained_sine_on_vector(half_sin1)
        put((0, 1), 0, CH, 6, held("y_first", [P, 2 * CH], F32))
        features(1, magnitudes(1), sine1)
        put((2,), 0, CH, 7, keep.tile([P, CH], F32, name="y0", tag="size1"))
        sine = gained_sine(half_sines(2))
        size = magnitudes(2)
        put((0,), CH, CH, 2, held("y1a", [P, CH], F32))
        features(2, size, sine)
        put((1, 2), CH, CH, 0, keep.tile([P, 2 * CH], F32, name="y1b", tag="size2"))
        sine = gained_sine(half_sines(3))
        size = magnitudes(3)
        put((0,), 2 * CH, CH, 2, held("y2a", [P, CH], F32))
        features(3, size, sine)
        put((1,), 2 * CH, CH, 1, keep.tile([P, CH], F32, name="y2b", tag="size3"))
        put((0,), 3 * CH, CH, 4, held("y3a", [P, CH], F32))
        put((1,), 3 * CH, CH, 6, held("y3b", [P, CH], F32))
        put((2,), 2 * CH, 2 * CH, 5, held("y4", [P, 2 * CH], F32))
